import numpy as np
import ml_dtypes


def mxq(x, axis, fmt="e4m3"):
    dtype, down = {"e4m3": (ml_dtypes.float8_e4m3fn, 7), "e5m2": (ml_dtypes.float8_e5m2, 14)}[fmt]
    v = np.moveaxis(np.asarray(x, np.float32).astype(ml_dtypes.bfloat16).astype(np.float64), axis, -1)
    blocks = v.reshape(v.shape[:-1] + (-1, 32))
    amax = np.abs(blocks).max(-1, keepdims=True)
    byte = np.maximum(np.where(amax > 0, np.frexp(amax)[1] - 1 + 127, 0) - down, 1)
    scale = np.exp2(byte - 127.0)
    codes = (blocks / scale).astype(np.float32).astype(dtype).astype(np.float64)
    return np.moveaxis((codes * scale).reshape(v.shape), -1, axis)


WIDE = False


def mx_kscale(k):
    if not WIDE:
        return np.ones(k)
    levels = np.array([10, -10, 5, -5, 0])
    if k % 512:
        return np.exp2(np.random.permutation(np.resize(levels, k // 32))).repeat(32)
    a = np.empty((k // 512, 16))
    for p in range(k // 512):
        a[p, :8] = np.random.permutation(np.resize(levels, 8))
        for g in range(8):
            far = levels[np.abs(levels - a[p, g]) >= 10]
            a[p, g + 8] = far[np.random.randint(len(far))]
    return np.exp2(a.ravel()).repeat(32)


def f64(x):
    return np.asarray(x).astype(np.float64)


def striped(idx):
    return np.tile(idx.reshape(-1, 16).T, (8, 1)).astype(np.uint16)


def unstriped(offs):
    return offs[:16].T.reshape(-1).astype(np.int64)


def pack_weight(w):
    k, n = w.shape
    w = f64(np.asarray(w, np.float32).astype(ml_dtypes.bfloat16)).reshape(k // 32, 32, n)
    amax = np.abs(w).max(1)
    byte = np.clip(np.where(amax > 0, np.frexp(amax)[1] - 1 + 127 - 7, 1), 1, 254)
    scaled = (w * np.exp2(127.0 - byte)[:, None, :]).reshape(k, n).astype(np.float32)
    words = np.ascontiguousarray(scaled.reshape(k // 512, 128, 4, n).transpose(0, 1, 3, 2)).astype(ml_dtypes.float8_e4m3fn).view(np.uint8)
    return words, np.ascontiguousarray(byte.astype(np.uint8).reshape(k // 512, 16, n))


def unpack_weight(words, scales):
    g, p, n, _ = words.shape
    vals = np.ascontiguousarray(words).view(ml_dtypes.float8_e4m3fn).astype(np.float64) * np.repeat(np.exp2(scales.astype(np.float64) - 127.0), 8, axis=1)[..., None]
    return vals.transpose(0, 1, 3, 2).reshape(g * 512, n)


def sigmoid(v):
    return 1.0 / (1.0 + np.exp(-np.maximum(v, -700.0)))


K, T, S, V = 512, 1024, 512, 512


def setup_inputs():
    n = np.random.standard_normal
    s = mx_kscale(K)[:, None]
    packed_xT = pack_weight(n((K, T)) * s)
    packed_eT = pack_weight(n((K, T)) * s)
    packed_dT = pack_weight(n((K, T)) * s)
    return {
        "x_words": packed_xT[0],
        "x_scales": packed_xT[1],
        "e_words": packed_eT[0],
        "e_scales": packed_eT[1],
        "d_words": packed_dT[0],
        "d_scales": packed_dT[1],
        "hT": (n((K, V)) / np.sqrt(K) / s).astype(np.float32),
        "gT": (n((K, V)) / np.sqrt(K) / s).astype(np.float32),
        "fT": (n((K, V)) / np.sqrt(K) / s).astype(np.float32),
        "offs": striped(np.random.permutation(T)[:S]),
    }


def reference(x_words, x_scales, e_words, e_scales, d_words, d_scales, hT, gT, fT, offs):
    fTq = mxq(f64(fT), 0, "e4m3")
    d_offs = unpack_weight(d_words, d_scales)[:, unstriped(offs)]
    gg = sigmoid(fTq.T @ d_offs)
    hTq = mxq(f64(hT), 0, "e4m3")
    xq = unpack_weight(x_words, x_scales)[:, unstriped(offs)]
    y = hTq.T @ xq
    gTq = mxq(f64(gT), 0, "e4m3")
    e_offs = unpack_weight(e_words, e_scales)[:, unstriped(offs)]
    z = gTq.T @ e_offs
    return gg * np.maximum(y, z)

@@ -1,0 +1,170 @@
+from contextlib import ExitStack
+
+import concourse.mybir as mybir
+
+K, T, S, V = 512, 1024, 512, 512
+FLOPS = 3 * 2 * K * S * V
+
+F32 = mybir.dt.float32
+BF16 = mybir.dt.bfloat16
+I32 = mybir.dt.int32
+U32 = mybir.dt.uint32
+U16 = mybir.dt.uint16
+U8 = mybir.dt.uint8
+FP8X4 = mybir.dt.float8_e4m3fn_x4
+ACT = mybir.ActivationFunctionType
+ALU = mybir.AluOpType
+
+P = 128
+PACK = 4
+
+HALF = 256
+
+
+def tile_picked_ymol_max_p_kernel(
+    tc, x_words, x_scales, e_words, e_scales, d_words, d_scales, hT, gT, fT, offs, out
+):
+    nc = tc.nc
+    words_in = {"x": x_words, "e": e_words, "d": d_words}
+    scales_in = {"x": x_scales, "e": e_scales, "d": d_scales}
+    users_in = {"x": hT, "e": gT, "d": fT}
+
+    with ExitStack() as ctx:
+        keep = ctx.enter_context(tc.tile_pool(name="keep", bufs=1))
+        psum = ctx.enter_context(tc.psum_pool(name="psum", bufs=1))
+
+        offsets = keep.tile([P, S // 16], U16, name="offsets")
+        nc.sync.dma_start(offsets[:], offs)
+
+        warm_in = keep.tile([P, 1], F32, name="warm_in")
+        warm_out = keep.tile([P, 1], F32, name="warm_out")
+        nc.vector.memset(warm_in[:], 0.0)
+        nc.scalar.activation(warm_out[:], warm_in[:], ACT.Sigmoid)
+
+        word_win, byte_win, word_got, byte_got = {}, {}, {}, {}
+        for n in "xed":
+            word_win[n] = keep.tile([P, T], U32, name="word_win_" + n, align_bytes=64)
+            byte_win[n] = keep.tile([P, T], U8, name="byte_win_" + n, align_bytes=64)
+            word_got[n] = keep.tile([P, S], U32, name="word_got_" + n, align_bytes=64)
+            byte_got[n] = keep.tile([P, S], U8, name="byte_got_" + n, align_bytes=64)
+            nc.vector.memset(byte_win[n][:].bitcast(I32), 0)
+
+        raw, grouped, codes, planes = {}, {}, {}, {}
+
+        def load_words(n):
+            nc.sync.dma_start(word_win[n][:].bitcast(I32), words_in[n][0].rearrange("p n t -> p (n t)").bitcast(I32))
+
+        def load_scales(n):
+            for q in range(4):
+                nc.sync.dma_start(
+                    byte_win[n][32 * q : 32 * q + 4, :].bitcast(I32), scales_in[n][0, 4 * q : 4 * q + 4, :].bitcast(I32)
+                )
+
+        def load_users(n, c):
+            raw[n, c] = keep.tile([P, PACK, HALF], F32, name="raw_%s%d" % (n, c))
+            src = users_in[n].rearrange("(p j) v -> p j v", j=PACK)
+            nc.sync.dma_start(raw[n, c][:], src[:, :, c * HALF : (c + 1) * HALF])
+
+        def gather_words(n):
+            nc.vector.tensor_copy(word_got[n][:], word_win[n][:].indirect(offsets[:]))
+
+        def gather_bytes(n):
+            nc.vector.tensor_copy(byte_got[n][:], byte_win[n][:].indirect(offsets[:]))
+
+        def cast(n, c):
+            grouped[n, c] = keep.tile([P, HALF * PACK], BF16, name="grouped_%s%d" % (n, c), align_bytes=64)
+            nc.scalar.copy(
+                grouped[n, c][:].rearrange("p (c i t) -> p c t i", i=4, t=PACK),
+                raw[n, c][:].rearrange("p t (c i) -> p c t i", i=4),
+            )
+
+        def quantize(n, c):
+            codes[n, c] = keep.tile([P, HALF], U32, name="codes_%s%d" % (n, c), align_bytes=64)
+            planes[n, c] = keep.tile([P, HALF], U8, name="planes_%s%d" % (n, c), align_bytes=64)
+            nc.vector.quantize_mx(out=codes[n, c][:].bitcast(FP8X4), scales=planes[n, c][:], in_=grouped[n, c][:])
+
+        banks = {}
+
+        def product(n, m):
+            c, cols = m // 2, slice((m % 2) * P, (m % 2 + 1) * P)
+            banks[n, m] = psum.tile([P, S], F32, name="bank_%s%d" % (n, m), tag="bank_%s%d" % (n, m % (2 if n == "x" else 3)))
+            nc.tensor.matmul_mx(
+                out=banks[n, m][:],
+                lhsT=codes[n, c][:, cols].bitcast(FP8X4),
+                lhsT_scale=planes[n, c][:, cols],
+                rhs=word_got[n][:].bitcast(FP8X4),
+                rhs_scale=byte_got[n][:],
+                start=True,
+                stop=True,
+            )
+
+        y_sb, best, gate = {}, {}, {}
+
+        def copy_y(m):
+            y_sb[m] = keep.tile([P, S], F32, name="y_sb%d" % m)
+            nc.scalar.copy(y_sb[m][:], banks["x", m][:])
+
+        def larger(m):
+            best[m] = keep.tile([P, S], F32, name="best%d" % m)
+            nc.vector.tensor_tensor(best[m][:], banks["e", m][:], y_sb[m][:], ALU.max)
+
+        def sigmoid(m):
+            gate[m] = keep.tile([P, S], F32, name="gate%d" % m)
+            nc.scalar.activation(gate[m][:], banks["d", m][:], ACT.Sigmoid)
+
+        def finish(m):
+            res = keep.tile([P, S], F32, name="res%d" % m)
+            nc.vector.tensor_tensor(res[:], best[m][:], gate[m][:], ALU.mult)
+            nc.sync.dma_start(out[m * P : (m + 1) * P, :], res[:])
+
+        load_users("x", 0)
+        load_scales("x")
+        load_words("x")
+        load_users("e", 0)
+        load_scales("e")
+        load_words("e")
+        load_scales("d")
+        load_users("d", 0)
+        load_words("d")
+        load_users("x", 1)
+        load_users("e", 1)
+        load_users("d", 1)
+
+        gather_bytes("x")
+        cast("x", 0)
+        gather_words("x")
+        cast("e", 0)
+        gather_bytes("e")
+        quantize("x", 0)
+        gather_words("e")
+        cast("d", 0)
+        quantize("e", 0)
+        gather_bytes("d")
+        for m in (0, 1):
+            product("x", m)
+            product("e", m)
+            copy_y(m)
+        gather_words("d")
+        quantize("d", 0)
+        cast("x", 1)
+        for m in (0, 1):
+            product("d", m)
+            larger(m)
+        cast("e", 1)
+        quantize("x", 1)
+        for m in (0, 1):
+            sigmoid(m)
+            finish(m)
+        cast("d", 1)
+        quantize("e", 1)
+        for m in (2, 3):
+            product("x", m)
+            product("e", m)
+            copy_y(m)
+        quantize("d", 1)
+        for m in (2, 3):
+            product("d", m)
+            larger(m)
+        for m in (2, 3):
+            sigmoid(m)
+            finish(m)

@@ -18,8 +18,6 @@ ALU = mybir.AluOpType
 P = 128
 PACK = 4
 
-HALF = 256
-
 
 def tile_picked_ymol_max_p_kernel(
     tc, x_words, x_scales, e_words, e_scales, d_words, d_scales, hT, gT, fT, offs, out
@@ -31,23 +29,33 @@ def tile_picked_ymol_max_p_kernel(
 
     with ExitStack() as ctx:
         keep = ctx.enter_context(tc.tile_pool(name="keep", bufs=1))
+        reuse = ctx.enter_context(tc.tile_pool(name="reuse", bufs=1))
         psum = ctx.enter_context(tc.psum_pool(name="psum", bufs=1))
 
         offsets = keep.tile([P, S // 16], U16, name="offsets")
         nc.sync.dma_start(offsets[:], offs)
 
-        warm_in = keep.tile([P, 1], F32, name="warm_in")
-        warm_out = keep.tile([P, 1], F32, name="warm_out")
-        nc.vector.memset(warm_in[:], 0.0)
-        nc.scalar.activation(warm_out[:], warm_in[:], ACT.Sigmoid)
+        place = {}
+        free = [0]
+
+        def tile(shape, dtype, name, nbytes, over=None, shift=0):
+            if over is None:
+                place[name] = free[0]
+                free[0] = free[0] + nbytes
+            else:
+                place[name] = place[over] + shift
+            return reuse.tile(shape, dtype, name=name, offset=place[name], align_bytes=64)
 
         word_win, byte_win, word_got, byte_got = {}, {}, {}, {}
-        for n in "xed":
-            word_win[n] = keep.tile([P, T], U32, name="word_win_" + n, align_bytes=64)
-            byte_win[n] = keep.tile([P, T], U8, name="byte_win_" + n, align_bytes=64)
-            word_got[n] = keep.tile([P, S], U32, name="word_got_" + n, align_bytes=64)
-            byte_got[n] = keep.tile([P, S], U8, name="byte_got_" + n, align_bytes=64)
+        for n in "dxe":
+            word_win[n] = tile([P, T], U32, "word_win_" + n, 4 * T)
+            byte_win[n] = tile([P, T], U8, "byte_win_" + n, T)
             nc.vector.memset(byte_win[n][:].bitcast(I32), 0)
+
+        warm_in = keep.tile([P, 1], F32, name="warm_in")
+        warm_out = keep.tile([P, 1], F32, name="warm_out")
+        nc.gpsimd.memset(warm_in[:], 0.0)
+        nc.scalar.activation(warm_out[:], warm_in[:], ACT.Sigmoid)
 
         raw, grouped, codes, planes = {}, {}, {}, {}
 
@@ -60,111 +68,129 @@ def tile_picked_ymol_max_p_kernel(
                     byte_win[n][32 * q : 32 * q + 4, :].bitcast(I32), scales_in[n][0, 4 * q : 4 * q + 4, :].bitcast(I32)
                 )
 
-        def load_users(n, c):
-            raw[n, c] = keep.tile([P, PACK, HALF], F32, name="raw_%s%d" % (n, c))
+        def load_users(n, m, tiles):
+            width = tiles * P
+            raw[n, m] = tile([P, PACK, width], F32, "raw_%s%d" % (n, m), 4 * PACK * width)
             src = users_in[n].rearrange("(p j) v -> p j v", j=PACK)
-            nc.sync.dma_start(raw[n, c][:], src[:, :, c * HALF : (c + 1) * HALF])
+            nc.sync.dma_start(raw[n, m][:], src[:, :, m * P : m * P + width])
 
-        def gather_words(n):
+        def gather_words(n, over=None):
+            word_got[n] = tile([P, S], U32, "word_got_" + n, 4 * S, over)
             nc.vector.tensor_copy(word_got[n][:], word_win[n][:].indirect(offsets[:]))
 
-        def gather_bytes(n):
+        def gather_bytes(n, over=None):
+            byte_got[n] = tile([P, S], U8, "byte_got_" + n, S, over)
             nc.vector.tensor_copy(byte_got[n][:], byte_win[n][:].indirect(offsets[:]))
 
-        def cast(n, c):
-            grouped[n, c] = keep.tile([P, HALF * PACK], BF16, name="grouped_%s%d" % (n, c), align_bytes=64)
+        def cast(n, m):
+            width = raw[n, m].shape[2]
+            grouped[n, m] = tile([P, width * PACK], BF16, "grouped_%s%d" % (n, m), 2 * PACK * width)
             nc.scalar.copy(
-                grouped[n, c][:].rearrange("p (c i t) -> p c t i", i=4, t=PACK),
-                raw[n, c][:].rearrange("p t (c i) -> p c t i", i=4),
+                grouped[n, m][:].rearrange("p (c i t) -> p c t i", i=4, t=PACK),
+                raw[n, m][:].rearrange("p t (c i) -> p c t i", i=4),
             )
 
-        def quantize(n, c):
-            codes[n, c] = keep.tile([P, HALF], U32, name="codes_%s%d" % (n, c), align_bytes=64)
-            planes[n, c] = keep.tile([P, HALF], U8, name="planes_%s%d" % (n, c), align_bytes=64)
-            nc.vector.quantize_mx(out=codes[n, c][:].bitcast(FP8X4), scales=planes[n, c][:], in_=grouped[n, c][:])
+        def quantize(n, m, over=None, shift=0):
+            width = raw[n, m].shape[2]
+            made = tile([P, width], U32, "codes_%s%d" % (n, m), 4 * width, over, shift)
+            plane = tile([P, width], U8, "planes_%s%d" % (n, m), width)
+            nc.vector.quantize_mx(out=made[:].bitcast(FP8X4), scales=plane[:], in_=grouped[n, m][:])
+            for i in range(width // P):
+                codes[n, m + i] = made[:, i * P : (i + 1) * P]
+                planes[n, m + i] = plane[:, i * P : (i + 1) * P]
 
         banks = {}
 
         def product(n, m):
-            c, cols = m // 2, slice((m % 2) * P, (m % 2 + 1) * P)
             banks[n, m] = psum.tile([P, S], F32, name="bank_%s%d" % (n, m), tag="bank_%s%d" % (n, m % (2 if n == "x" else 3)))
             nc.tensor.matmul_mx(
                 out=banks[n, m][:],
-                lhsT=codes[n, c][:, cols].bitcast(FP8X4),
-                lhsT_scale=planes[n, c][:, cols],
+                lhsT=codes[n, m].bitcast(FP8X4),
+                lhsT_scale=planes[n, m],
                 rhs=word_got[n][:].bitcast(FP8X4),
                 rhs_scale=byte_got[n][:],
                 start=True,
                 stop=True,
             )
 
-        y_sb, best, gate = {}, {}, {}
+        y_sb, best, gate, res = {}, {}, {}, {}
 
-        def copy_y(m):
-            y_sb[m] = keep.tile([P, S], F32, name="y_sb%d" % m)
+        def copy_y(m, over=None, shift=0):
+            y_sb[m] = tile([P, S], F32, "y_sb%d" % m, 4 * S, over, shift)
             nc.scalar.copy(y_sb[m][:], banks["x", m][:])
 
-        def larger(m):
-            best[m] = keep.tile([P, S], F32, name="best%d" % m)
+        def larger(m, over=None):
+            best[m] = tile([P, S], F32, "best%d" % m, 4 * S, over)
             nc.vector.tensor_tensor(best[m][:], banks["e", m][:], y_sb[m][:], ALU.max)
 
-        def sigmoid(m):
-            gate[m] = keep.tile([P, S], F32, name="gate%d" % m)
+        def sigmoid(m, over=None, shift=0):
+            gate[m] = tile([P, S], F32, "gate%d" % m, 4 * S, over, shift)
             nc.scalar.activation(gate[m][:], banks["d", m][:], ACT.Sigmoid)
 
-        def finish(m):
-            res = keep.tile([P, S], F32, name="res%d" % m)
-            nc.vector.tensor_tensor(res[:], best[m][:], gate[m][:], ALU.mult)
-            nc.sync.dma_start(out[m * P : (m + 1) * P, :], res[:])
+        def finish(m, shares):
+            res[m] = tile([P, S], F32, "res%d" % m, 4 * S)
+            for engine, cols in shares:
+                engine.tensor_tensor(res[m][:, cols], best[m][:, cols], gate[m][:, cols], ALU.mult)
+            nc.sync.dma_start(out[m * P : (m + 1) * P, :], res[m][:])
 
-        load_users("x", 0)
+        load_words("d")
+        load_users("d", 0, 2)
+        load_scales("d")
+        load_users("x", 0, 2)
+        load_users("e", 0, 2)
         load_scales("x")
         load_words("x")
-        load_users("e", 0)
+        load_users("x", 2, 2)
         load_scales("e")
+        load_users("e", 2, 2)
         load_words("e")
-        load_scales("d")
-        load_users("d", 0)
-        load_words("d")
-        load_users("x", 1)
-        load_users("e", 1)
-        load_users("d", 1)
+        load_users("d", 2, 1)
+        load_users("d", 3, 1)
 
-        gather_bytes("x")
-        cast("x", 0)
-        gather_words("x")
-        cast("e", 0)
-        gather_bytes("e")
-        quantize("x", 0)
-        gather_words("e")
-        cast("d", 0)
-        quantize("e", 0)
-        gather_bytes("d")
-        for m in (0, 1):
-            product("x", m)
-            product("e", m)
-            copy_y(m)
         gather_words("d")
-        quantize("d", 0)
-        cast("x", 1)
+        cast("d", 0)
+        gather_bytes("d")
+        quantize("d", 0, "byte_win_d")
+        cast("x", 0)
+        cast("e", 0)
+        gather_bytes("x", "grouped_d0")
+        gather_words("x")
+        quantize("x", 0)
+        quantize("e", 0, "byte_win_x")
         for m in (0, 1):
             product("d", m)
-            larger(m)
-        cast("e", 1)
-        quantize("x", 1)
-        for m in (0, 1):
-            sigmoid(m)
-            finish(m)
-        cast("d", 1)
-        quantize("e", 1)
-        for m in (2, 3):
-            product("x", m)
-            product("e", m)
-            copy_y(m)
-        quantize("d", 1)
-        for m in (2, 3):
-            product("d", m)
-            larger(m)
-        for m in (2, 3):
-            sigmoid(m)
-            finish(m)
+            sigmoid(m, "raw_e0", m * 4 * S)
+        cast("x", 2)
+        cast("e", 2)
+        gather_bytes("e", "word_win_x")
+        gather_words("e")
+        quantize("x", 2, "word_win_e")
+        quantize("e", 2, "word_win_e", 1024)
+        product("x", 0)
+        product("x", 1)
+        copy_y(0, "raw_e2")
+        cast("d", 2)
+        cast("d", 3)
+        quantize("d", 2, "word_win_e", 2048)
+        quantize("d", 3, "word_win_e", 2560)
+        copy_y(1, "raw_d3")
+        product("e", 0)
+        product("x", 2)
+        product("e", 1)
+        product("d", 2)
+        product("x", 3)
+        product("e", 2)
+        product("d", 3)
+        larger(0, "grouped_d2")
+        larger(1)
+        product("e", 3)
+        copy_y(2)
+        sigmoid(2)
+        copy_y(3)
+        sigmoid(3)
+        larger(2)
+        larger(3)
+        finish(0, [(nc.gpsimd, slice(0, S))])
+        finish(1, [(nc.gpsimd, slice(0, S // 2)), (nc.vector, slice(S // 2, S))])
+        finish(2, [(nc.vector, slice(0, S))])
+        finish(3, [(nc.vector, slice(0, S))])

@@ -49,7 +49,7 @@ def tile_picked_ymol_max_p_kernel(
         word_win, byte_win, word_got, byte_got = {}, {}, {}, {}
         for n in "dxe":
             word_win[n] = tile([P, T], U32, "word_win_" + n, 4 * T)
-            byte_win[n] = tile([P, T], U8, "byte_win_" + n, T)
+            byte_win[n] = tile([P, T], U8, "byte_win_" + n, 2 * T)
             nc.vector.memset(byte_win[n][:].bitcast(I32), 0)
 
         warm_in = keep.tile([P, 1], F32, name="warm_in")
@@ -59,8 +59,11 @@ def tile_picked_ymol_max_p_kernel(
 
         raw, grouped, codes, planes = {}, {}, {}, {}
 
-        def load_words(n):
-            nc.sync.dma_start(word_win[n][:].bitcast(I32), words_in[n][0].rearrange("p n t -> p (n t)").bitcast(I32))
+        def load_words(n, parts=1):
+            src = words_in[n][0].rearrange("p n t -> p (n t)").bitcast(I32)
+            for i in range(parts):
+                cols = slice(i * T // parts, (i + 1) * T // parts)
+                nc.sync.dma_start(word_win[n][:, cols].bitcast(I32), src[:, cols])
 
         def load_scales(n):
             for q in range(4):
@@ -68,9 +71,9 @@ def tile_picked_ymol_max_p_kernel(
                     byte_win[n][32 * q : 32 * q + 4, :].bitcast(I32), scales_in[n][0, 4 * q : 4 * q + 4, :].bitcast(I32)
                 )
 
-        def load_users(n, m, tiles):
+        def load_users(n, m, tiles, spare=0):
             width = tiles * P
-            raw[n, m] = tile([P, PACK, width], F32, "raw_%s%d" % (n, m), 4 * PACK * width)
+            raw[n, m] = tile([P, PACK, width], F32, "raw_%s%d" % (n, m), 4 * PACK * width + spare)
             src = users_in[n].rearrange("(p j) v -> p j v", j=PACK)
             nc.sync.dma_start(raw[n, m][:], src[:, :, m * P : m * P + width])
 
@@ -78,26 +81,28 @@ def tile_picked_ymol_max_p_kernel(
             word_got[n] = tile([P, S], U32, "word_got_" + n, 4 * S, over)
             nc.vector.tensor_copy(word_got[n][:], word_win[n][:].indirect(offsets[:]))
 
-        def gather_bytes(n, over=None):
-            byte_got[n] = tile([P, S], U8, "byte_got_" + n, S, over)
+        def gather_bytes(n, over=None, shift=0):
+            byte_got[n] = tile([P, S], U8, "byte_got_" + n, S, over, shift)
             nc.vector.tensor_copy(byte_got[n][:], byte_win[n][:].indirect(offsets[:]))
 
-        def cast(n, m):
-            width = raw[n, m].shape[2]
-            grouped[n, m] = tile([P, width * PACK], BF16, "grouped_%s%d" % (n, m), 2 * PACK * width)
+        def cast(n, m, into):
             nc.scalar.copy(
-                grouped[n, m][:].rearrange("p (c i t) -> p c t i", i=4, t=PACK),
+                into.rearrange("p (c i t) -> p c t i", i=4, t=PACK),
                 raw[n, m][:].rearrange("p t (c i) -> p c t i", i=4),
             )
 
-        def quantize(n, m, over=None, shift=0):
-            width = raw[n, m].shape[2]
-            made = tile([P, width], U32, "codes_%s%d" % (n, m), 4 * width, over, shift)
-            plane = tile([P, width], U8, "planes_%s%d" % (n, m), width)
-            nc.vector.quantize_mx(out=made[:].bitcast(FP8X4), scales=plane[:], in_=grouped[n, m][:])
-            for i in range(width // P):
-                codes[n, m + i] = made[:, i * P : (i + 1) * P]
-                planes[n, m + i] = plane[:, i * P : (i + 1) * P]
+        def staging(name, tiles):
+            return tile([P, tiles * P * PACK], BF16, name, 2 * PACK * P * tiles)
+
+        def quantize(stage, keys, over=None):
+            width = len(keys) * P
+            name = "%s%d" % keys[0]
+            made = tile([P, width], U32, "codes_" + name, 4 * width, over)
+            plane = tile([P, width], U8, "planes_" + name, width)
+            nc.vector.quantize_mx(out=made[:].bitcast(FP8X4), scales=plane[:], in_=stage[:])
+            for i, key in enumerate(keys):
+                codes[key] = made[:, i * P : (i + 1) * P]
+                planes[key] = plane[:, i * P : (i + 1) * P]
 
         banks = {}
 
@@ -113,84 +118,96 @@ def tile_picked_ymol_max_p_kernel(
                 stop=True,
             )
 
-        y_sb, best, gate, res = {}, {}, {}, {}
+        y_sb, best, gate = {}, {}, {}
 
-        def copy_y(m, over=None, shift=0):
-            y_sb[m] = tile([P, S], F32, "y_sb%d" % m, 4 * S, over, shift)
-            nc.scalar.copy(y_sb[m][:], banks["x", m][:])
+        def group(name, slots, over, shift=0):
+            together = tile([P, len(slots), S], F32, name, 4 * S * len(slots), over, shift)
+            for i, (store, m) in enumerate(slots):
+                store[m] = together[:, i, :]
 
-        def larger(m, over=None):
-            best[m] = tile([P, S], F32, "best%d" % m, 4 * S, over)
-            nc.vector.tensor_tensor(best[m][:], banks["e", m][:], y_sb[m][:], ALU.max)
+        def copy_y(m):
+            nc.scalar.copy(y_sb[m], banks["x", m][:])
 
-        def sigmoid(m, over=None, shift=0):
-            gate[m] = tile([P, S], F32, "gate%d" % m, 4 * S, over, shift)
-            nc.scalar.activation(gate[m][:], banks["d", m][:], ACT.Sigmoid)
+        def larger(m):
+            nc.vector.tensor_tensor(best[m], banks["e", m][:], y_sb[m], ALU.max)
 
-        def finish(m, shares):
-            res[m] = tile([P, S], F32, "res%d" % m, 4 * S)
-            for engine, cols in shares:
-                engine.tensor_tensor(res[m][:, cols], best[m][:, cols], gate[m][:, cols], ALU.mult)
-            nc.sync.dma_start(out[m * P : (m + 1) * P, :], res[m][:])
+        def sigmoid(m):
+            nc.scalar.activation(gate[m], banks["d", m][:], ACT.Sigmoid)
 
-        load_words("d")
-        load_users("d", 0, 2)
+        def finish(m, cols, engine, over=None):
+            width = cols.stop - cols.start
+            part = tile([P, width], F32, "res%d_%d" % (m, cols.start), 4 * width, over)
+            engine.tensor_tensor(part[:], best[m][:, cols], gate[m][:, cols], ALU.mult)
+            nc.sync.dma_start(out[m * P : (m + 1) * P, cols], part[:])
+
+        load_words("d", 2)
         load_scales("d")
+        load_users("d", 0, 2)
         load_users("x", 0, 2)
-        load_users("e", 0, 2)
         load_scales("x")
+        load_users("e", 0, 2)
         load_words("x")
         load_users("x", 2, 2)
         load_scales("e")
         load_users("e", 2, 2)
         load_words("e")
         load_users("d", 2, 1)
-        load_users("d", 3, 1)
+        load_users("d", 3, 1, 5 * 4 * S)
 
+        half = 2 * P * PACK
         gather_words("d")
-        cast("d", 0)
+        stage_f = staging("stage_f", 2)
+        cast("d", 0, stage_f[:])
         gather_bytes("d")
-        quantize("d", 0, "byte_win_d")
-        cast("x", 0)
-        cast("e", 0)
-        gather_bytes("x", "grouped_d0")
+        quantize(stage_f, [("d", 0), ("d", 1)], "byte_win_d")
+        stage_a = staging("stage_a", 4)
+        cast("x", 0, stage_a[:, :half])
+        cast("e", 0, stage_a[:, half:])
+        gather_bytes("x", "stage_f")
         gather_words("x")
-        quantize("x", 0)
-        quantize("e", 0, "byte_win_x")
+        quantize(stage_a, [("x", 0), ("x", 1), ("e", 0), ("e", 1)], "word_win_x")
+        group("early", [(gate, 0), (gate, 1)], "raw_e0", -1024)
         for m in (0, 1):
             product("d", m)
-            sigmoid(m, "raw_e0", m * 4 * S)
-        cast("x", 2)
-        cast("e", 2)
-        gather_bytes("e", "word_win_x")
+            sigmoid(m)
+        stage_b = staging("stage_b", 4)
+        cast("x", 2, stage_b[:, :half])
+        cast("e", 2, stage_b[:, half:])
+        gather_bytes("e", "raw_e0", 3072)
         gather_words("e")
-        quantize("x", 2, "word_win_e")
-        quantize("e", 2, "word_win_e", 1024)
+        quantize(stage_b, [("x", 2), ("x", 3), ("e", 2), ("e", 3)], "word_win_e")
         product("x", 0)
         product("x", 1)
-        copy_y(0, "raw_e2")
-        cast("d", 2)
-        cast("d", 3)
-        quantize("d", 2, "word_win_e", 2048)
-        quantize("d", 3, "word_win_e", 2560)
-        copy_y(1, "raw_d3")
+        group("middle", [(y_sb, 0)], "raw_e2")
+        copy_y(0)
+        for m in (2, 3):
+            stage_t = staging("stage_t%d" % m, 1)
+            cast("d", m, stage_t[:])
+            quantize(stage_t, [("d", m)])
+        group("late", [(y_sb, 1), (y_sb, 2), (y_sb, 3), (gate, 2), (gate, 3), (best, 0)], "raw_d3")
+        for m in (1, 2, 3):
+            group("best%d" % m, [(best, m)], None)
+        copy_y(1)
         product("e", 0)
         product("x", 2)
         product("e", 1)
-        product("d", 2)
         product("x", 3)
+        product("d", 2)
         product("e", 2)
         product("d", 3)
-        larger(0, "grouped_d2")
+        larger(0)
         larger(1)
         product("e", 3)
         copy_y(2)
-        sigmoid(2)
         copy_y(3)
+        sigmoid(2)
         sigmoid(3)
         larger(2)
         larger(3)
-        finish(0, [(nc.gpsimd, slice(0, S))])
-        finish(1, [(nc.gpsimd, slice(0, S // 2)), (nc.vector, slice(S // 2, S))])
-        finish(2, [(nc.vector, slice(0, S))])
-        finish(3, [(nc.vector, slice(0, S))])
+        whole, left, right = slice(0, S), slice(0, S // 2), slice(S // 2, S)
+        finish(0, whole, nc.gpsimd)
+        finish(1, left, nc.gpsimd)
+        finish(2, whole, nc.vector)
+        finish(3, left, nc.vector)
+        finish(1, right, nc.vector, "best2")
+        finish(3, right, nc.vector)

from contextlib import ExitStack

import concourse.mybir as mybir

K, T, S, V = 512, 1024, 512, 512
FLOPS = 3 * 2 * K * S * V

F32 = mybir.dt.float32
BF16 = mybir.dt.bfloat16
I32 = mybir.dt.int32
U32 = mybir.dt.uint32
U16 = mybir.dt.uint16
U8 = mybir.dt.uint8
FP8X4 = mybir.dt.float8_e4m3fn_x4
ACT = mybir.ActivationFunctionType
ALU = mybir.AluOpType

P = 128
PACK = 4


def tile_picked_ymol_max_p_kernel(
    tc, x_words, x_scales, e_words, e_scales, d_words, d_scales, hT, gT, fT, offs, out
):
    nc = tc.nc
    words_in = {"x": x_words, "e": e_words, "d": d_words}
    scales_in = {"x": x_scales, "e": e_scales, "d": d_scales}
    users_in = {"x": hT, "e": gT, "d": fT}

    with ExitStack() as ctx:
        keep = ctx.enter_context(tc.tile_pool(name="keep", bufs=1))
        reuse = ctx.enter_context(tc.tile_pool(name="reuse", bufs=1))
        psum = ctx.enter_context(tc.psum_pool(name="psum", bufs=1))

        offsets = keep.tile([P, S // 16], U16, name="offsets")
        nc.sync.dma_start(offsets[:], offs)

        place = {}
        free = [0]

        def tile(shape, dtype, name, nbytes, over=None, shift=0):
            if over is None:
                place[name] = free[0]
                free[0] = free[0] + nbytes
            else:
                place[name] = place[over] + shift
            return reuse.tile(shape, dtype, name=name, offset=place[name], align_bytes=64)

        word_win, byte_win, word_got, byte_got = {}, {}, {}, {}
        for n in "dxe":
            word_win[n] = tile([P, T], U32, "word_win_" + n, 4 * T)
            byte_win[n] = tile([P, T], U8, "byte_win_" + n, 2 * T)
            nc.vector.memset(byte_win[n][:].bitcast(I32), 0)

        warm_in = keep.tile([P, 1], F32, name="warm_in")
        warm_out = keep.tile([P, 1], F32, name="warm_out")
        nc.gpsimd.memset(warm_in[:], 0.0)
        nc.scalar.activation(warm_out[:], warm_in[:], ACT.Sigmoid)

        raw, grouped, codes, planes = {}, {}, {}, {}

        def load_words(n, parts=1):
            src = words_in[n][0].rearrange("p n t -> p (n t)").bitcast(I32)
            for i in range(parts):
                cols = slice(i * T // parts, (i + 1) * T // parts)
                nc.sync.dma_start(word_win[n][:, cols].bitcast(I32), src[:, cols])

        def load_scales(n):
            for q in range(4):
                nc.sync.dma_start(
                    byte_win[n][32 * q : 32 * q + 4, :].bitcast(I32), scales_in[n][0, 4 * q : 4 * q + 4, :].bitcast(I32)
                )

        def load_users(n, m, tiles, spare=0):
            width = tiles * P
            raw[n, m] = tile([P, PACK, width], F32, "raw_%s%d" % (n, m), 4 * PACK * width + spare)
            src = users_in[n].rearrange("(p j) v -> p j v", j=PACK)
            nc.sync.dma_start(raw[n, m][:], src[:, :, m * P : m * P + width])

        def gather_words(n, over=None):
            word_got[n] = tile([P, S], U32, "word_got_" + n, 4 * S, over)
            nc.vector.tensor_copy(word_got[n][:], word_win[n][:].indirect(offsets[:]))

        def gather_bytes(n, over=None, shift=0):
            byte_got[n] = tile([P, S], U8, "byte_got_" + n, S, over, shift)
            nc.vector.tensor_copy(byte_got[n][:], byte_win[n][:].indirect(offsets[:]))

        def cast(n, m, into):
            nc.scalar.copy(
                into.rearrange("p (c i t) -> p c t i", i=4, t=PACK),
                raw[n, m][:].rearrange("p t (c i) -> p c t i", i=4),
            )

        def staging(name, tiles):
            return tile([P, tiles * P * PACK], BF16, name, 2 * PACK * P * tiles)

        def quantize(stage, keys, over=None):
            width = len(keys) * P
            name = "%s%d" % keys[0]
            made = tile([P, width], U32, "codes_" + name, 4 * width, over)
            plane = tile([P, width], U8, "planes_" + name, width)
            nc.vector.quantize_mx(out=made[:].bitcast(FP8X4), scales=plane[:], in_=stage[:])
            for i, key in enumerate(keys):
                codes[key] = made[:, i * P : (i + 1) * P]
                planes[key] = plane[:, i * P : (i + 1) * P]

        banks = {}

        def product(n, m):
            banks[n, m] = psum.tile([P, S], F32, name="bank_%s%d" % (n, m), tag="bank_%s%d" % (n, m % (2 if n == "x" else 3)))
            nc.tensor.matmul_mx(
                out=banks[n, m][:],
                lhsT=codes[n, m].bitcast(FP8X4),
                lhsT_scale=planes[n, m],
                rhs=word_got[n][:].bitcast(FP8X4),
                rhs_scale=byte_got[n][:],
                start=True,
                stop=True,
            )

        y_sb, best, gate = {}, {}, {}

        def group(name, slots, over, shift=0):
            together = tile([P, len(slots), S], F32, name, 4 * S * len(slots), over, shift)
            for i, (store, m) in enumerate(slots):
                store[m] = together[:, i, :]

        def copy_y(m):
            nc.scalar.copy(y_sb[m], banks["x", m][:])

        def larger(m):
            nc.vector.tensor_tensor(best[m], banks["e", m][:], y_sb[m], ALU.max)

        def sigmoid(m):
            nc.scalar.activation(gate[m], banks["d", m][:], ACT.Sigmoid)

        def finish(m, cols, engine, over=None):
            width = cols.stop - cols.start
            part = tile([P, width], F32, "res%d_%d" % (m, cols.start), 4 * width, over)
            engine.tensor_tensor(part[:], best[m][:, cols], gate[m][:, cols], ALU.mult)
            nc.sync.dma_start(out[m * P : (m + 1) * P, cols], part[:])

        load_words("d", 2)
        load_scales("d")
        load_users("d", 0, 2)
        load_users("x", 0, 2)
        load_scales("x")
        load_users("e", 0, 2)
        load_words("x")
        load_users("x", 2, 2)
        load_scales("e")
        load_users("e", 2, 2)
        load_words("e")
        load_users("d", 2, 1)
        load_users("d", 3, 1, 5 * 4 * S)

        half = 2 * P * PACK
        gather_words("d")
        stage_f = staging("stage_f", 2)
        cast("d", 0, stage_f[:])
        gather_bytes("d")
        quantize(stage_f, [("d", 0), ("d", 1)], "byte_win_d")
        stage_a = staging("stage_a", 4)
        cast("x", 0, stage_a[:, :half])
        cast("e", 0, stage_a[:, half:])
        gather_bytes("x", "stage_f")
        gather_words("x")
        quantize(stage_a, [("x", 0), ("x", 1), ("e", 0), ("e", 1)], "word_win_x")
        group("early", [(gate, 0), (gate, 1)], "raw_e0", -1024)
        for m in (0, 1):
            product("d", m)
            sigmoid(m)
        stage_b = staging("stage_b", 4)
        cast("x", 2, stage_b[:, :half])
        cast("e", 2, stage_b[:, half:])
        gather_bytes("e", "raw_e0", 3072)
        gather_words("e")
        quantize(stage_b, [("x", 2), ("x", 3), ("e", 2), ("e", 3)], "word_win_e")
        product("x", 0)
        product("x", 1)
        group("middle", [(y_sb, 0)], "raw_e2")
        copy_y(0)
        for m in (2, 3):
            stage_t = staging("stage_t%d" % m, 1)
            cast("d", m, stage_t[:])
            quantize(stage_t, [("d", m)])
        group("late", [(y_sb, 1), (y_sb, 2), (y_sb, 3), (gate, 2), (gate, 3), (best, 0)], "raw_d3")
        for m in (1, 2, 3):
            group("best%d" % m, [(best, m)], None)
        copy_y(1)
        product("e", 0)
        product("x", 2)
        product("e", 1)
        product("x", 3)
        product("d", 2)
        product("e", 2)
        product("d", 3)
        larger(0)
        larger(1)
        product("e", 3)
        copy_y(2)
        copy_y(3)
        sigmoid(2)
        sigmoid(3)
        larger(2)
        larger(3)
        whole, left, right = slice(0, S), slice(0, S // 2), slice(S // 2, S)
        finish(0, whole, nc.gpsimd)
        finish(1, left, nc.gpsimd)
        finish(2, whole, nc.vector)
        finish(3, left, nc.vector)
        finish(1, right, nc.vector, "best2")
        finish(3, right, nc.vector)
